import numpy as np
import ml_dtypes


def mxq(x, axis, fmt="e4m3"):
    dtype, down = {"e4m3": (ml_dtypes.float8_e4m3fn, 7), "e5m2": (ml_dtypes.float8_e5m2, 14)}[fmt]
    v = np.moveaxis(np.asarray(x, np.float32).astype(ml_dtypes.bfloat16).astype(np.float64), axis, -1)
    blocks = v.reshape(v.shape[:-1] + (-1, 32))
    amax = np.abs(blocks).max(-1, keepdims=True)
    byte = np.maximum(np.where(amax > 0, np.frexp(amax)[1] - 1 + 127, 0) - down, 1)
    scale = np.exp2(byte - 127.0)
    codes = (blocks / scale).astype(np.float32).astype(dtype).astype(np.float64)
    return np.moveaxis((codes * scale).reshape(v.shape), -1, axis)


WIDE = False


def mx_kscale(k):
    if not WIDE:
        return np.ones(k)
    levels = np.array([10, -10, 5, -5, 0])
    if k % 512:
        return np.exp2(np.random.permutation(np.resize(levels, k // 32))).repeat(32)
    a = np.empty((k // 512, 16))
    for p in range(k // 512):
        a[p, :8] = np.random.permutation(np.resize(levels, 8))
        for g in range(8):
            far = levels[np.abs(levels - a[p, g]) >= 10]
            a[p, g + 8] = far[np.random.randint(len(far))]
    return np.exp2(a.ravel()).repeat(32)


def f64(x):
    return np.asarray(x).astype(np.float64)


def striped(idx):
    return np.tile(idx.reshape(-1, 16).T, (8, 1)).astype(np.uint16)


def unstriped(offs):
    return offs[:16].T.reshape(-1).astype(np.int64)


E2M1 = np.array([0.0, 0.5, 1.0, 1.5, 2.0, 3.0, 4.0, 6.0, -0.0, -0.5, -1.0, -1.5, -2.0, -3.0, -4.0, -6.0])


def pack_weight(w, fmt):
    k, n = w.shape
    w = f64(np.asarray(w, np.float32).astype(ml_dtypes.bfloat16)).reshape(k // 32, 32, n)
    amax = np.abs(w).max(1)
    if fmt == "e4m3":
        byte = np.frexp(amax)[1] - 1 + 127 - 7
    else:
        mant, ex = np.frexp(amax / 6.0)
        byte = np.where(mant > 0.5, ex, ex - 1) + 127
    byte = np.clip(np.where(amax > 0, byte, 1), 1, 254)
    scaled = (w * np.exp2(127.0 - byte)[:, None, :]).reshape(k, n).astype(np.float32)
    by_word = np.ascontiguousarray(scaled.reshape(k // 512, 128, 4, n).transpose(0, 1, 3, 2))
    if fmt == "e4m3":
        words = by_word.astype(ml_dtypes.float8_e4m3fn).view(np.uint8)
    else:
        c = by_word.astype(ml_dtypes.float4_e2m1fn).view(np.uint8) & 0xF
        words = (c[..., 0::2] | (c[..., 1::2] << 4)).reshape(k // 512, 128, 2 * n)
    return np.ascontiguousarray(words), np.ascontiguousarray(byte.astype(np.uint8).reshape(k // 512, 16, n))


def unpack_weight(words, scales, fmt):
    g, _, n = scales.shape
    words = np.ascontiguousarray(words).reshape(g, 128, n, -1)
    if fmt == "e4m3":
        vals = words.view(ml_dtypes.float8_e4m3fn).astype(np.float64)
    else:
        nib = np.empty((g, 128, n, 4), np.uint8)
        nib[..., 0::2] = words & 0xF
        nib[..., 1::2] = words >> 4
        vals = E2M1[nib]
    vals = vals * np.repeat(np.exp2(scales.astype(np.float64) - 127.0), 8, axis=1)[..., None]
    return vals.transpose(0, 1, 3, 2).reshape(g * 512, n)


def gelu(v):
    return 0.5 * v * (1.0 + np.tanh(np.sqrt(2.0 / np.pi) * (v + 0.044715 * v**3)))


def bf(x):
    return np.asarray(x, np.float32).astype(ml_dtypes.bfloat16)


def planes(Y):
    n, m = Y.shape
    b = f64(bf(Y)).reshape(n // 32, 32, m)
    amax = np.abs(b).max(1)
    byte = np.clip(np.where(amax > 0, np.frexp(amax)[1] - 1 + 127 - 7, 1), 1, 254)
    codes = (b * np.exp2(127.0 - byte)[:, None, :]).reshape(n, m).astype(np.float32).astype(ml_dtypes.float8_e4m3fn).view(np.uint8)
    words = codes.reshape(n // 512, 128, 4, m).transpose(0, 1, 3, 2)
    return np.ascontiguousarray(words), np.ascontiguousarray(byte.astype(np.uint8).reshape(n // 512, 16, m))


T, S, T2, P, K, H, N = 4096, 1024, 2048, 1024, 1536, 1024, 384

def setup_inputs():
    n = np.random.standard_normal
    s = mx_kscale(K)[:, None]
    u = mx_kscale(H)[:, None]
    d = {}
    d["tab_words"], d["tab_scales"] = pack_weight(n((K, T)) * s, "e4m3")
    d["offs"] = striped(np.random.permutation(T)[:S])
    d["offs2"] = striped(np.random.permutation(T2)[:S])
    d["offs3"] = striped(np.random.permutation(T2)[:P])
    d["w1"] = (n((K, H)) / K ** 0.5 / s * u.T).astype(np.float32)
    d["side"] = np.exp(0.4 * n((H, S))).astype(np.float32)
    d["wgs"] = np.exp(0.3 * n((128, S))).astype(np.float32)
    d["page0"] = (n((H, T2)) * u).astype(np.float32)
    d["slope"] = (1.4 * np.exp(0.4 * n(H)) / u[:, 0]).astype(np.float32)
    d["swell"] = (1.5 * np.exp(0.3 * n(H)) * u[:, 0]).astype(np.float32)
    d["w2"] = (0.6 * n((H, N)) / H ** 0.5 / u).astype(np.float32)
    d["w3_words"], d["w3_scales"] = pack_weight(0.6 * n((H, N)) / H ** 0.5 / u, "e2m1")
    d["lift"] = (0.8 * n(N)).astype(np.float32)
    return d

def reference(tab_words, tab_scales, offs, offs2, offs3, w1, side, wgs, page0, slope, swell, w2, w3_words, w3_scales, lift):
    v = unpack_weight(tab_words, tab_scales, "e4m3")[:, unstriped(offs)]
    h = (mxq(f64(w1), 0, "e4m3").T @ v) * f64(side)
    page = f64(page0).copy()
    page[:, unstriped(offs2)] = np.tile(f64(wgs), (H // 128, 1)) * h
    r = page[:, unstriped(offs3)]
    x = r + f64(swell)[:, None] * np.tanh(f64(slope)[:, None] * r)
    xq = mxq(x, 0, "e4m3")
    first = mxq(f64(w2), 0, "e4m3").T @ xq
    second = unpack_weight(w3_words, w3_scales, "e2m1").T @ xq
    y = first - np.maximum(second, f64(lift)[:, None])
    words, scales = planes(page)
    return y, page, words, scales

@@ -1,0 +1,376 @@
+from contextlib import ExitStack
+
+import concourse.mybir as mybir
+
+T, S, T2, PICK, K, H, N = 4096, 1024, 2048, 1024, 1536, 1024, 384
+FLOPS = 2 * K * H * S + 2 * 2 * H * N * PICK
+
+F32 = mybir.dt.float32
+BF16 = mybir.dt.bfloat16
+I32 = mybir.dt.int32
+U32 = mybir.dt.uint32
+U16 = mybir.dt.uint16
+U8 = mybir.dt.uint8
+FP8X4 = mybir.dt.float8_e4m3fn_x4
+FP4X4 = mybir.dt.float4_e2m1fn_x4
+ALU = mybir.AluOpType
+ACT = mybir.ActivationFunctionType
+
+P = 128
+PACK = 4
+PASS = P * PACK
+BANK = 512
+K_PASSES = K // PASS
+GROUPS = H // PASS
+SLICES = GROUPS * PACK
+N_TILES = N // P
+HALVES = 2
+QUADS = 4
+QUAD = 32
+H_TAGS = ("h0", "h1", "h0", "h3", "h0", "h1", "h6", "h1")
+
+
+def tile_list_groove_noise_page_kernel(
+    tc, tab_words, tab_scales, offs, offs2, offs3, w1, side, wgs, page0, slope, swell, w2, w3_words, w3_scales, lift,
+    out_0, out_1, out_2, out_3,
+):
+    nc = tc.nc
+    side_rows = side.rearrange("(g p t) j -> g t p j", p=P, t=PACK)
+    page0_rows = page0.rearrange("(g p t) m -> g t p m", p=P, t=PACK)
+    out_1_rows = out_1.rearrange("(g p t) m -> g t p m", p=P, t=PACK)
+    wgs_rows = wgs.rearrange("(q t) j -> t q j", t=PACK)
+
+    with ExitStack() as ctx:
+        lists = ctx.enter_context(tc.tile_pool(name="lists", bufs=1))
+        keep = ctx.enter_context(tc.tile_pool(name="keep", bufs=1))
+        ring = ctx.enter_context(tc.tile_pool(name="ring", bufs=2))
+        psum = ctx.enter_context(tc.psum_pool(name="psum", bufs=1))
+
+        idx = lists.tile([P, S // 16], U16, name="idx")
+        idx2 = lists.tile([P, S // 16], U16, name="idx2")
+        idx3 = lists.tile([P, PICK // 16], U16, name="idx3")
+
+        def half(h):
+            return slice(h * BANK, (h + 1) * BANK)
+
+        def list_half(h):
+            return slice(h * BANK // 16, (h + 1) * BANK // 16)
+
+        tab_sc = keep.tile([P, T], U8, name="tab_sc", align_bytes=64)
+        w3_sc = keep.tile([P, GROUPS, N], U8, name="w3_sc", align_bytes=64)
+        nc.vector.memset(tab_sc[:].bitcast(I32), 0)
+        nc.vector.memset(w3_sc[:].bitcast(I32), 0)
+        for q in range(QUADS):
+            nc.gpsimd.dma_start(
+                out=tab_sc[QUAD * q : QUAD * q + 4 * K_PASSES, :].bitcast(I32),
+                in_=tab_scales[:, 4 * q : 4 * q + 4, :].bitcast(I32),
+            )
+        slope_t = keep.tile([P, GROUPS, PACK], F32, name="slope_t")
+        swell_t = keep.tile([P, GROUPS, PACK], F32, name="swell_t")
+        lift_t = keep.tile([P, N_TILES], F32, name="lift_t")
+        neg_lift = keep.tile([P, N_TILES], F32, name="neg_lift")
+
+        w1_raw, w1_codes, w1_sc = {}, {}, {}
+
+        def load_w1(g, a):
+            w1_raw[g, a] = ring.tile([P, PACK, PASS], F32, name="w_raw", tag="w_raw", bufs=3)
+            rows = w1[a * PASS : (a + 1) * PASS, g * PASS : (g + 1) * PASS]
+            nc.sync.dma_start(out=w1_raw[g, a][:], in_=rows.rearrange("(p i) r -> p i r", i=PACK))
+
+        w1_bf = {}
+
+        def round_w1(g, a):
+            w1_bf[g, a] = ring.tile([P, PASS * PACK], BF16, name="w_bf", tag="w_bf", bufs=3, align_bytes=64)
+            nc.scalar.copy(
+                out=w1_bf[g, a][:].rearrange("p (t q i) -> p q i t", t=PACK, i=PACK),
+                in_=w1_raw[g, a][:].rearrange("p i (q t) -> p q i t", t=PACK),
+            )
+
+        def quantize_w1(g, a):
+            if a == 0:
+                tag = "w1_codes0" if g == 0 else "h3"
+                w1_codes[g] = keep.tile([P, K_PASSES * PASS], U32, name=f"w1_codes{g}", tag=tag, align_bytes=64)
+                w1_sc[g] = keep.tile([P, K_PASSES * PASS], U8, name=f"w1_sc{g}", align_bytes=64)
+            cols = slice(a * PASS, (a + 1) * PASS)
+            nc.vector.quantize_mx(out=w1_codes[g][:, cols].bitcast(FP8X4), scales=w1_sc[g][:, cols], in_=w1_bf[g, a][:])
+
+        side_t, page_t = {}, {}
+        wgs_t = [keep.tile([P, S], F32, name=f"wgs{t}") for t in range(PACK)]
+
+        def load_side(s, cols):
+            if s not in side_t:
+                side_t[s] = ring.tile([P, S], F32, name="side_t", tag="side_t", bufs=3)
+            nc.sync.dma_start(out=side_t[s][:, cols], in_=side_rows[s // PACK, s % PACK][:, cols])
+
+        def load_wgs(t, cols):
+            for q in range(QUADS):
+                nc.sync.dma_start(out=wgs_t[t][QUAD * q : QUAD * (q + 1), cols], in_=wgs_rows[t][:, cols])
+
+        def load_page(s):
+            page_t[s] = ring.tile([P, T2], F32, name="page", tag="page", bufs=4, align_bytes=64)
+            nc.sync.dma_start(out=page_t[s][:], in_=page0_rows[s // PACK, s % PACK])
+
+        def load_slice(s):
+            load_side(s, slice(0, S))
+            if s < PACK:
+                load_wgs(s, slice(0, S))
+            load_page(s)
+
+        load_w1(0, 0)
+        nc.sync.dma_start(idx[:], offs)
+        nc.sync.dma_start(idx2[:], offs2)
+        nc.sync.dma_start(idx3[:], offs3)
+        load_w1(0, 1)
+        load_w1(0, 2)
+        tab_w = []
+        for a in range(K_PASSES):
+            tab_w.append(keep.tile([P, T], I32, name=f"tab_w{a}", tag=f"big{a}", align_bytes=64))
+            nc.sync.dma_start(out=tab_w[a][:], in_=tab_words[a].rearrange("p t i -> p (t i)").bitcast(I32))
+        load_side(0, half(0))
+        load_wgs(0, half(0))
+        load_page(0)
+        load_side(0, half(1))
+        load_wgs(0, half(1))
+
+        v_sc = keep.tile([P, S], U8, name="v_sc", align_bytes=64)
+        nc.vector.tensor_copy(v_sc[:], tab_sc[:].indirect(idx[:]))
+        for a in range(K_PASSES):
+            round_w1(0, a)
+            quantize_w1(0, a)
+        v_w = [keep.tile([P, S], U32, name=f"v_w{a}", align_bytes=64) for a in range(K_PASSES)]
+        for a in range(K_PASSES - 1):
+            nc.vector.tensor_copy(v_w[a][:], tab_w[a][:].bitcast(U32).indirect(idx[:]))
+
+        banks = [None] * 8
+
+        def new_bank(b):
+            banks[b] = psum.tile([P, BANK], F32, name=f"bank{b}", tag=f"bank{b}")
+            return banks[b]
+
+        h_t = {}
+
+        def product(s, h):
+            g, t = divmod(s, PACK)
+            if s not in h_t:
+                h_t[s] = keep.tile([P, S], F32, name=f"h{s}", tag=H_TAGS[s], align_bytes=64)
+            acc = new_bank(2 * (s % 2) + h)
+            for a in range(K_PASSES):
+                nc.tensor.matmul_mx(
+                    out=acc[:],
+                    lhsT=w1_codes[g][:, a * PASS + t * P : a * PASS + (t + 1) * P].bitcast(FP8X4),
+                    lhsT_scale=w1_sc[g][:, a * PASS + t * P : a * PASS + (t + 1) * P],
+                    rhs=v_w[a][:, half(h)].bitcast(FP8X4),
+                    rhs_scale=v_sc[4 * a : P, half(h)],
+                    start=(a == 0),
+                    stop=(a == K_PASSES - 1),
+                )
+            nc.vector.tensor_tensor(h_t[s][:, half(h)], acc[:], side_t[s][:, half(h)], ALU.mult)
+
+        def scatter(s, cols, list_cols):
+            nc.vector.tensor_tensor(
+                page_t[s][:].indirect(idx2[:, list_cols]), h_t[s][:, cols], wgs_t[s % PACK][:, cols], ALU.mult
+            )
+
+        picked, bent, page_bf = {}, {}, {}
+
+        def fetch(s, cols, list_cols):
+            g, t = divmod(s, PACK)
+            if g not in picked:
+                picked[g] = keep.tile([P, PACK, PICK], F32, name=f"picked{g}", tag="big0", align_bytes=64)
+                bent[g] = keep.tile([P, PACK, PICK], F32, name=f"bent{g}", tag="big1", align_bytes=64)
+            nc.vector.tensor_copy(picked[g][:, t, cols], page_t[s][:].indirect(idx3[:, list_cols]))
+            nc.scalar.activation(bent[g][:, t, cols], picked[g][:, t, cols], ACT.Tanh, scale=slope_t[:, g, t : t + 1])
+            nc.scalar.activation(bent[g][:, t, cols], bent[g][:, t, cols], ACT.Copy, scale=swell_t[:, g, t : t + 1])
+
+        HALF_T2 = T2 // 2
+        pairs = {}
+
+        def round_page(s, h):
+            g, t = divmod(s, PACK)
+            if (g, h) not in pairs:
+                pairs[g, h] = keep.tile([P, HALF_T2 * PACK], BF16, name=f"pairs{g}{h}", tag=f"pairs{h}", align_bytes=64)
+            by_pair = pairs[g, h][:].rearrange("p (u m e) -> p u m e", u=2, e=2)
+            nc.scalar.copy(out=by_pair[:, t // 2, :, t % 2], in_=page_t[s][:, h * HALF_T2 : (h + 1) * HALF_T2])
+
+        def weave_page(g, h):
+            if g not in page_bf:
+                page_bf[g] = keep.tile([P, T2 * PACK], BF16, name=f"page_bf{g}", tag="big2", align_bytes=64)
+            woven = page_bf[g][:, h * HALF_T2 * PACK : (h + 1) * HALF_T2 * PACK]
+            nc.scalar.copy(
+                out=woven.bitcast(F32).rearrange("p (c i u) -> p c u i", i=2, u=2),
+                in_=pairs[g, h][:].bitcast(F32).rearrange("p (u c i) -> p c u i", u=2, i=2),
+            )
+
+        y_codes, y_sc = {}, {}
+
+        def page_planes(g, h):
+            if g not in y_codes:
+                if g == 0:
+                    y_codes[g] = keep.tile([P, T2], I32, name="y_codes0", tag="h0", align_bytes=64)
+                else:
+                    y_codes[g] = ring.tile([P, T2], I32, name="y_codes1", tag="page", bufs=4, align_bytes=64)
+                y_sc[g] = keep.tile([P, T2], U8, name=f"y_sc{g}", tag="y_sc", align_bytes=64)
+            cols = slice(h * HALF_T2, (h + 1) * HALF_T2)
+            nc.vector.quantize_mx(
+                out=y_codes[g][:, cols].bitcast(FP8X4),
+                scales=y_sc[g][:, cols],
+                in_=page_bf[g][:, h * HALF_T2 * PACK : (h + 1) * HALF_T2 * PACK],
+            )
+            nc.sync.dma_start(
+                out=out_2[g].rearrange("p m t -> p (m t)").bitcast(I32)[:, cols], in_=y_codes[g][:, cols]
+            )
+            if h == 1:
+                for q in range(QUADS):
+                    nc.sync.dma_start(
+                        out=out_3[g, 4 * q : 4 * q + 4, :].bitcast(I32),
+                        in_=y_sc[g][QUAD * q : QUAD * q + 4, :].bitcast(I32),
+                    )
+
+        x_codes = [keep.tile([P, PICK], U32, name=f"x_codes{g}", align_bytes=64) for g in range(GROUPS)]
+        x_sc = [keep.tile([P, PICK], U8, name=f"x_sc{g}", align_bytes=64) for g in range(GROUPS)]
+
+        x_bf = {}
+
+        def make_x(g, h):
+            if g not in x_bf:
+                x_bf[g] = keep.tile([P, PICK * PACK], BF16, name=f"x_bf{g}", tag="h0", align_bytes=64)
+            nc.vector.tensor_tensor(
+                x_bf[g][:, h * BANK * PACK : (h + 1) * BANK * PACK].rearrange("p (c i t) -> p c t i", i=2, t=PACK),
+                picked[g][:, :, half(h)].rearrange("p t (c i) -> p c t i", i=2),
+                bent[g][:, :, half(h)].rearrange("p t (c i) -> p c t i", i=2),
+                ALU.add,
+            )
+
+        def quantize_x(g, h):
+            nc.vector.quantize_mx(
+                out=x_codes[g][:, half(h)].bitcast(FP8X4),
+                scales=x_sc[g][:, half(h)],
+                in_=x_bf[g][:, h * BANK * PACK : (h + 1) * BANK * PACK],
+            )
+
+        w2_codes = []
+        w2_sc = keep.tile([P, GROUPS * N], U8, name="w2_sc", align_bytes=64)
+        w3_w = keep.tile([P, GROUPS, 2 * N], U8, name="w3_w", align_bytes=64)
+        w2_bf = keep.tile([P, GROUPS * N * PACK], BF16, name="w2_bf", align_bytes=64)
+
+        def prepare_w2_w3():
+            for g in range(GROUPS):
+                raw = ring.tile([P, PACK, N], F32, name="w_raw", tag="w_raw", bufs=3)
+                nc.sync.dma_start(out=raw[:], in_=w2[g * PASS : (g + 1) * PASS, :].rearrange("(p i) n -> p i n", i=PACK))
+                nc.scalar.copy(
+                    out=w2_bf[:, g * N * PACK : (g + 1) * N * PACK].rearrange("p (c n i) -> p c i n", n=4, i=PACK),
+                    in_=raw[:].rearrange("p i (c n) -> p c i n", n=4),
+                )
+            nc.sync.dma_start(out=w3_w[:].bitcast(I32), in_=w3_words.bitcast(I32).rearrange("g p w -> p g w"))
+            with nc.allow_non_contiguous_dma(reason="one value of lift a partition"):
+                nc.sync.dma_start(out=lift_t[:], in_=lift.rearrange("(c p) -> p c", p=P))
+            for q in range(QUADS):
+                nc.sync.dma_start(
+                    out=w3_sc[QUAD * q : QUAD * q + 4, :, :].bitcast(I32),
+                    in_=w3_scales[:, 4 * q : 4 * q + 4, :].bitcast(I32).rearrange("g r n -> r g n"),
+                )
+
+        def quantize_w2():
+            w2_codes.append(keep.tile([P, GROUPS * N], U32, name="w2_codes", tag="h6", align_bytes=64))
+            for lo, hi in ((0, 512), (512, 768)):
+                nc.vector.quantize_mx(
+                    out=w2_codes[0][:, lo:hi].bitcast(FP8X4), scales=w2_sc[:, lo:hi], in_=w2_bf[:, lo * PACK : hi * PACK]
+                )
+
+        def score_pass(acc, which, c, h, g):
+            if which == 0:
+                cols = slice(g * N + c * P, g * N + (c + 1) * P)
+                lhsT, lhsT_scale = w2_codes[0][:, cols].bitcast(FP8X4), w2_sc[:, cols]
+            else:
+                lhsT = w3_w[:, g, 2 * c * P : 2 * (c + 1) * P].bitcast(FP4X4)
+                lhsT_scale = w3_sc[:, g, c * P : (c + 1) * P]
+            nc.tensor.matmul_mx(
+                out=acc[:], lhsT=lhsT, lhsT_scale=lhsT_scale,
+                rhs=x_codes[g][:, half(h)].bitcast(FP8X4), rhs_scale=x_sc[g][:, half(h)],
+                start=(g == 0), stop=(g == GROUPS - 1),
+            )
+
+        def score_out(c, h, first, second):
+            neg_second = ring.tile([P, BANK], F32, name="neg_second", tag="w_raw", bufs=3)
+            nc.scalar.activation(neg_second[:], second[:], ACT.Copy, scale=-1.0)
+            y = ring.tile([P, BANK], F32, name="y", tag="side_t", bufs=3)
+            nc.vector.scalar_tensor_tensor(
+                out=y[:], in0=neg_second[:], scalar=neg_lift[:, c : c + 1], in1=first[:], op0=ALU.min, op1=ALU.add
+            )
+            nc.sync.dma_start(out=out_0[c * P : (c + 1) * P, half(h)], in_=y[:])
+
+        last = K_PASSES - 1
+        for h in range(HALVES):
+            nc.vector.tensor_copy(v_w[last][:, half(h)], tab_w[last][:].bitcast(U32).indirect(idx[:, list_half(h)]))
+            product(0, h)
+        nc.sync.dma_start(out=slope_t[:], in_=slope.rearrange("(g p t) -> p g t", p=P, t=PACK))
+        nc.sync.dma_start(out=swell_t[:], in_=swell.rearrange("(g p t) -> p g t", p=P, t=PACK))
+        load_slice(1)
+        load_w1(1, 0)
+        round_w1(1, 0)
+        load_slice(2)
+        for a in range(1, K_PASSES):
+            load_w1(1, a)
+            round_w1(1, a)
+
+        tiles = [(c, h) for h in range(HALVES) for c in range(N_TILES)]
+        sums = {}
+        whole, whole_list = slice(0, S), slice(0, S // 16)
+        for s in range(SLICES):
+            g, t = divmod(s, PACK)
+            if s == 0:
+                for h in range(HALVES):
+                    scatter(s, half(h), list_half(h))
+            else:
+                scatter(s, whole, whole_list)
+            if s + 3 < SLICES:
+                load_slice(s + 3)
+            nc.sync.dma_start(out=out_1_rows[g, t], in_=page_t[s][:])
+            if s == 2:
+                prepare_w2_w3()
+                nc.vector.tensor_scalar(out=neg_lift[:], in0=lift_t[:], scalar1=-1.0, scalar2=None, op0=ALU.mult)
+            if s == PACK - 1:
+                for a in range(K_PASSES):
+                    quantize_w1(1, a)
+            if s == PACK:
+                for h in range(HALVES):
+                    make_x(0, h)
+                for h in range(HALVES):
+                    quantize_x(0, h)
+                for h in range(HALVES):
+                    page_planes(0, h)
+            if s == SLICES - 2:
+                quantize_w2()
+            if s + 1 < SLICES:
+                for h in range(HALVES):
+                    product(s + 1, h)
+            if s == SLICES - 2:
+                for i, (c, h) in enumerate(tiles[:4]):
+                    for which in range(2):
+                        sums[c, h, which] = new_bank((4 + 2 * i + which) % 8)
+                        score_pass(sums[c, h, which], which, c, h, 0)
+            if s + 1 < SLICES:
+                fetch(s, whole, whole_list)
+                for h in range(HALVES):
+                    round_page(s, h)
+            if s == PACK - 1:
+                for h in range(HALVES):
+                    weave_page(0, h)
+
+        s, g = SLICES - 1, GROUPS - 1
+        for h in range(HALVES):
+            fetch(s, half(h), list_half(h))
+        for h in range(HALVES):
+            make_x(g, h)
+            quantize_x(g, h)
+        for i, (c, h) in enumerate(tiles):
+            for which in range(2):
+                if i >= 4:
+                    sums[c, h, which] = new_bank((4 + 2 * i + which) % 8)
+                    score_pass(sums[c, h, which], which, c, h, 0)
+                score_pass(sums[c, h, which], which, c, h, 1)
+            score_out(c, h, sums[c, h, 0], sums[c, h, 1])
+            if i in (0, 2):
+                round_page(s, i // 2)
+                weave_page(g, i // 2)
+                page_planes(g, i // 2)

@@ -60,11 +60,6 @@ def tile_list_groove_noise_page_kernel(
         w3_sc = keep.tile([P, GROUPS, N], U8, name="w3_sc", align_bytes=64)
         nc.vector.memset(tab_sc[:].bitcast(I32), 0)
         nc.vector.memset(w3_sc[:].bitcast(I32), 0)
-        for q in range(QUADS):
-            nc.gpsimd.dma_start(
-                out=tab_sc[QUAD * q : QUAD * q + 4 * K_PASSES, :].bitcast(I32),
-                in_=tab_scales[:, 4 * q : 4 * q + 4, :].bitcast(I32),
-            )
         slope_t = keep.tile([P, GROUPS, PACK], F32, name="slope_t")
         swell_t = keep.tile([P, GROUPS, PACK], F32, name="swell_t")
         lift_t = keep.tile([P, N_TILES], F32, name="lift_t")
@@ -117,6 +112,11 @@ def tile_list_groove_noise_page_kernel(
             load_page(s)
 
         load_w1(0, 0)
+        for q in range(QUADS):
+            nc.sync.dma_start(
+                out=tab_sc[QUAD * q : QUAD * q + 4 * K_PASSES, :].bitcast(I32),
+                in_=tab_scales[:, 4 * q : 4 * q + 4, :].bitcast(I32),
+            )
         nc.sync.dma_start(idx[:], offs)
         nc.sync.dma_start(idx2[:], offs2)
         nc.sync.dma_start(idx3[:], offs3)
@@ -164,12 +164,21 @@ def tile_list_groove_noise_page_kernel(
                     start=(a == 0),
                     stop=(a == K_PASSES - 1),
                 )
-            nc.vector.tensor_tensor(h_t[s][:, half(h)], acc[:], side_t[s][:, half(h)], ALU.mult)
+            if t == 0:
+                nc.vector.tensor_tensor(h_t[s][:, half(h)], acc[:], side_t[s][:, half(h)], ALU.mult)
+                return
+            if h == 0:
+                nc.gpsimd.tensor_tensor(side_t[s][:], side_t[s][:], wgs_t[t][:], ALU.mult)
+            nc.scalar.copy(out=h_t[s][:, half(h)], in_=acc[:])
+            if h == 1:
+                nc.gpsimd.tensor_tensor(h_t[s][:], h_t[s][:], side_t[s][:], ALU.mult)
 
         def scatter(s, cols, list_cols):
-            nc.vector.tensor_tensor(
-                page_t[s][:].indirect(idx2[:, list_cols]), h_t[s][:, cols], wgs_t[s % PACK][:, cols], ALU.mult
-            )
+            window = page_t[s][:].indirect(idx2[:, list_cols])
+            if s % PACK == 0:
+                nc.vector.tensor_tensor(window, h_t[s][:, cols], wgs_t[0][:, cols], ALU.mult)
+            else:
+                nc.vector.tensor_copy(window, h_t[s][:, cols])
 
         picked, bent, page_bf = {}, {}, {}
 

@@ -1,6 +1,7 @@
 from contextlib import ExitStack
 
 import concourse.mybir as mybir
+from concourse.masks import make_identity
 
 T, S, T2, PICK, K, H, N = 4096, 1024, 2048, 1024, 1536, 1024, 384
 FLOPS = 2 * K * H * S + 2 * 2 * H * N * PICK
@@ -27,7 +28,7 @@ N_TILES = N // P
 HALVES = 2
 QUADS = 4
 QUAD = 32
-H_TAGS = ("h0", "h1", "h0", "h3", "h0", "h1", "h6", "h1")
+H_TAGS = ("h0", "h1", "h2", "h3", "h0", "h1", "big2", "h3")
 
 
 def tile_list_groove_noise_page_kernel(
@@ -38,7 +39,6 @@ def tile_list_groove_noise_page_kernel(
     side_rows = side.rearrange("(g p t) j -> g t p j", p=P, t=PACK)
     page0_rows = page0.rearrange("(g p t) m -> g t p m", p=P, t=PACK)
     out_1_rows = out_1.rearrange("(g p t) m -> g t p m", p=P, t=PACK)
-    wgs_rows = wgs.rearrange("(q t) j -> t q j", t=PACK)
 
     with ExitStack() as ctx:
         lists = ctx.enter_context(tc.tile_pool(name="lists", bufs=1))
@@ -56,14 +56,13 @@ def tile_list_groove_noise_page_kernel(
         def list_half(h):
             return slice(h * BANK // 16, (h + 1) * BANK // 16)
 
-        tab_sc = keep.tile([P, T], U8, name="tab_sc", align_bytes=64)
+        tab_sc = keep.tile([P, T], U8, name="tab_sc", tag="h3", align_bytes=64)
         w3_sc = keep.tile([P, GROUPS, N], U8, name="w3_sc", align_bytes=64)
         nc.vector.memset(tab_sc[:].bitcast(I32), 0)
         nc.vector.memset(w3_sc[:].bitcast(I32), 0)
         slope_t = keep.tile([P, GROUPS, PACK], F32, name="slope_t")
         swell_t = keep.tile([P, GROUPS, PACK], F32, name="swell_t")
         lift_t = keep.tile([P, N_TILES], F32, name="lift_t")
-        neg_lift = keep.tile([P, N_TILES], F32, name="neg_lift")
 
         w1_raw, w1_codes, w1_sc = {}, {}, {}
 
@@ -72,45 +71,39 @@ def tile_list_groove_noise_page_kernel(
             rows = w1[a * PASS : (a + 1) * PASS, g * PASS : (g + 1) * PASS]
             nc.sync.dma_start(out=w1_raw[g, a][:], in_=rows.rearrange("(p i) r -> p i r", i=PACK))
 
-        w1_bf = {}
-
-        def round_w1(g, a):
-            w1_bf[g, a] = ring.tile([P, PASS * PACK], BF16, name="w_bf", tag="w_bf", bufs=3, align_bytes=64)
+        def round_w1(g, a, grouped):
             nc.scalar.copy(
-                out=w1_bf[g, a][:].rearrange("p (t q i) -> p q i t", t=PACK, i=PACK),
+                out=grouped.rearrange("p (t q i) -> p q i t", t=PACK, i=PACK),
                 in_=w1_raw[g, a][:].rearrange("p i (q t) -> p q i t", t=PACK),
             )
 
-        def quantize_w1(g, a):
+        def quantize_w1(g, a, grouped):
             if a == 0:
-                tag = "w1_codes0" if g == 0 else "h3"
+                tag = "w1_codes0" if g == 0 else "h2"
                 w1_codes[g] = keep.tile([P, K_PASSES * PASS], U32, name=f"w1_codes{g}", tag=tag, align_bytes=64)
                 w1_sc[g] = keep.tile([P, K_PASSES * PASS], U8, name=f"w1_sc{g}", align_bytes=64)
-            cols = slice(a * PASS, (a + 1) * PASS)
-            nc.vector.quantize_mx(out=w1_codes[g][:, cols].bitcast(FP8X4), scales=w1_sc[g][:, cols], in_=w1_bf[g, a][:])
+            cols = slice(a * PASS, a * PASS + grouped.shape[1] // PACK)
+            nc.vector.quantize_mx(out=w1_codes[g][:, cols].bitcast(FP8X4), scales=w1_sc[g][:, cols], in_=grouped)
 
         side_t, page_t = {}, {}
         wgs_t = [keep.tile([P, S], F32, name=f"wgs{t}") for t in range(PACK)]
 
-        def load_side(s, cols):
-            if s not in side_t:
-                side_t[s] = ring.tile([P, S], F32, name="side_t", tag="side_t", bufs=3)
-            nc.sync.dma_start(out=side_t[s][:, cols], in_=side_rows[s // PACK, s % PACK][:, cols])
-
-        def load_wgs(t, cols):
-            for q in range(QUADS):
-                nc.sync.dma_start(out=wgs_t[t][QUAD * q : QUAD * (q + 1), cols], in_=wgs_rows[t][:, cols])
+        def load_side(s):
+            side_t[s] = ring.tile([P, S], F32, name="side_t", tag="side_t", bufs=4)
+            nc.sync.dma_start(out=side_t[s][:], in_=side_rows[s // PACK, s % PACK])
 
         def load_page(s):
             page_t[s] = ring.tile([P, T2], F32, name="page", tag="page", bufs=4, align_bytes=64)
             nc.sync.dma_start(out=page_t[s][:], in_=page0_rows[s // PACK, s % PACK])
 
-        def load_slice(s):
-            load_side(s, slice(0, S))
-            if s < PACK:
-                load_wgs(s, slice(0, S))
-            load_page(s)
+        banks = [None] * 8
 
+        def new_bank(b):
+            banks[b] = psum.tile([P, BANK], F32, name=f"bank{b}", tag=f"bank{b}")
+            return banks[b]
+
+        wgs_raw = keep.tile([P, S], F32, name="wgs_raw", tag="h6", align_bytes=64)
+        nc.sync.dma_start(out=wgs_raw[:], in_=wgs)
         load_w1(0, 0)
         for q in range(QUADS):
             nc.sync.dma_start(
@@ -124,28 +117,43 @@ def tile_list_groove_noise_page_kernel(
         load_w1(0, 2)
         tab_w = []
         for a in range(K_PASSES):
+            if a == K_PASSES - 1:
+                load_side(0)
             tab_w.append(keep.tile([P, T], I32, name=f"tab_w{a}", tag=f"big{a}", align_bytes=64))
             nc.sync.dma_start(out=tab_w[a][:], in_=tab_words[a].rearrange("p t i -> p (t i)").bitcast(I32))
-        load_side(0, half(0))
-        load_wgs(0, half(0))
         load_page(0)
-        load_side(0, half(1))
-        load_wgs(0, half(1))
 
-        v_sc = keep.tile([P, S], U8, name="v_sc", align_bytes=64)
+        ident = keep.tile([P, P], F32, name="ident")
+        make_identity(nc, ident[:])
+        turned = []
+        for h in range(HALVES):
+            acc = new_bank(4 + h)
+            for b in range(4):
+                nc.tensor.transpose(acc[:, b * P : (b + 1) * P], wgs_raw[:, h * BANK + b * P : h * BANK + (b + 1) * P], ident[:])
+            turned.append(keep.tile([P, 4 * PACK * P], F32, name=f"turned{h}", tag=f"pairs{h}", align_bytes=64))
+            for b in range(4):
+                rows = acc[:, b * P : (b + 1) * P].rearrange("p (q t) -> p t q", t=PACK)
+                nc.vector.tensor_copy(
+                    turned[h][:, b * PASS : (b + 1) * PASS].rearrange("p (t r q) -> p t r q", t=PACK, r=QUADS),
+                    rows.unsqueeze(2).broadcast_to([P, PACK, QUADS, QUAD]),
+                )
+
+        v_sc = keep.tile([P, S], U8, name="v_sc", tag="v_sc", align_bytes=64)
         nc.vector.tensor_copy(v_sc[:], tab_sc[:].indirect(idx[:]))
         for a in range(K_PASSES):
-            round_w1(0, a)
-            quantize_w1(0, a)
+            grouped = ring.tile([P, PASS * PACK], BF16, name="w_bf", tag="w_bf", align_bytes=64)
+            round_w1(0, a, grouped[:])
+            quantize_w1(0, a, grouped[:])
+        for t in range(PACK):
+            for h in range(HALVES):
+                acc = new_bank(4 + (2 + HALVES * t + h) % 4)
+                for b in range(4):
+                    cols = slice(b * PASS + t * P, b * PASS + (t + 1) * P)
+                    nc.tensor.transpose(acc[:, b * P : (b + 1) * P], turned[h][:, cols], ident[:])
+                nc.scalar.copy(out=wgs_t[t][:, half(h)], in_=acc[:])
         v_w = [keep.tile([P, S], U32, name=f"v_w{a}", align_bytes=64) for a in range(K_PASSES)]
         for a in range(K_PASSES - 1):
             nc.vector.tensor_copy(v_w[a][:], tab_w[a][:].bitcast(U32).indirect(idx[:]))
-
-        banks = [None] * 8
-
-        def new_bank(b):
-            banks[b] = psum.tile([P, BANK], F32, name=f"bank{b}", tag=f"bank{b}")
-            return banks[b]
 
         h_t = {}
 
@@ -164,21 +172,16 @@ def tile_list_groove_noise_page_kernel(
                     start=(a == 0),
                     stop=(a == K_PASSES - 1),
                 )
-            if t == 0:
+            if s == 0:
                 nc.vector.tensor_tensor(h_t[s][:, half(h)], acc[:], side_t[s][:, half(h)], ALU.mult)
                 return
-            if h == 0:
-                nc.gpsimd.tensor_tensor(side_t[s][:], side_t[s][:], wgs_t[t][:], ALU.mult)
             nc.scalar.copy(out=h_t[s][:, half(h)], in_=acc[:])
             if h == 1:
+                nc.gpsimd.tensor_tensor(h_t[s][:], h_t[s][:], wgs_t[t][:], ALU.mult)
                 nc.gpsimd.tensor_tensor(h_t[s][:], h_t[s][:], side_t[s][:], ALU.mult)
 
         def scatter(s, cols, list_cols):
-            window = page_t[s][:].indirect(idx2[:, list_cols])
-            if s % PACK == 0:
-                nc.vector.tensor_tensor(window, h_t[s][:, cols], wgs_t[0][:, cols], ALU.mult)
-            else:
-                nc.vector.tensor_copy(window, h_t[s][:, cols])
+            nc.vector.tensor_copy(page_t[s][:].indirect(idx2[:, list_cols]), h_t[s][:, cols])
 
         picked, bent, page_bf = {}, {}, {}
 
@@ -260,16 +263,21 @@ def tile_list_groove_noise_page_kernel(
         w2_codes = []
         w2_sc = keep.tile([P, GROUPS * N], U8, name="w2_sc", align_bytes=64)
         w3_w = keep.tile([P, GROUPS, 2 * N], U8, name="w3_w", align_bytes=64)
-        w2_bf = keep.tile([P, GROUPS * N * PACK], BF16, name="w2_bf", align_bytes=64)
+        w2_raw, w2_bf = [], []
+
+        def round_w2():
+            w2_bf.append(keep.tile([P, GROUPS * N * PACK], BF16, name="w2_bf", tag="h0", align_bytes=64))
+            for g in range(GROUPS):
+                nc.scalar.copy(
+                    out=w2_bf[0][:, g * N * PACK : (g + 1) * N * PACK].rearrange("p (c n i) -> p c i n", n=4, i=PACK),
+                    in_=w2_raw[g][:].rearrange("p i (c n) -> p c i n", n=4),
+                )
 
         def prepare_w2_w3():
             for g in range(GROUPS):
-                raw = ring.tile([P, PACK, N], F32, name="w_raw", tag="w_raw", bufs=3)
-                nc.sync.dma_start(out=raw[:], in_=w2[g * PASS : (g + 1) * PASS, :].rearrange("(p i) n -> p i n", i=PACK))
-                nc.scalar.copy(
-                    out=w2_bf[:, g * N * PACK : (g + 1) * N * PACK].rearrange("p (c n i) -> p c i n", n=4, i=PACK),
-                    in_=raw[:].rearrange("p i (c n) -> p c i n", n=4),
-                )
+                w2_raw.append(ring.tile([P, PACK, N], F32, name="w_raw", tag="w_raw", bufs=3))
+                rows = w2[g * PASS : (g + 1) * PASS, :]
+                nc.sync.dma_start(out=w2_raw[g][:], in_=rows.rearrange("(p i) n -> p i n", i=PACK))
             nc.sync.dma_start(out=w3_w[:].bitcast(I32), in_=w3_words.bitcast(I32).rearrange("g p w -> p g w"))
             with nc.allow_non_contiguous_dma(reason="one value of lift a partition"):
                 nc.sync.dma_start(out=lift_t[:], in_=lift.rearrange("(c p) -> p c", p=P))
@@ -283,7 +291,7 @@ def tile_list_groove_noise_page_kernel(
             w2_codes.append(keep.tile([P, GROUPS * N], U32, name="w2_codes", tag="h6", align_bytes=64))
             for lo, hi in ((0, 512), (512, 768)):
                 nc.vector.quantize_mx(
-                    out=w2_codes[0][:, lo:hi].bitcast(FP8X4), scales=w2_sc[:, lo:hi], in_=w2_bf[:, lo * PACK : hi * PACK]
+                    out=w2_codes[0][:, lo:hi].bitcast(FP8X4), scales=w2_sc[:, lo:hi], in_=w2_bf[0][:, lo * PACK : hi * PACK]
                 )
 
         def score_pass(acc, which, c, h, g):
@@ -302,28 +310,33 @@ def tile_list_groove_noise_page_kernel(
         def score_out(c, h, first, second):
             neg_second = ring.tile([P, BANK], F32, name="neg_second", tag="w_raw", bufs=3)
             nc.scalar.activation(neg_second[:], second[:], ACT.Copy, scale=-1.0)
-            y = ring.tile([P, BANK], F32, name="y", tag="side_t", bufs=3)
+            y = ring.tile([P, BANK], F32, name="y", tag="side_t", bufs=4)
             nc.vector.scalar_tensor_tensor(
                 out=y[:], in0=neg_second[:], scalar=neg_lift[:, c : c + 1], in1=first[:], op0=ALU.min, op1=ALU.add
             )
             nc.sync.dma_start(out=out_0[c * P : (c + 1) * P, half(h)], in_=y[:])
 
         last = K_PASSES - 1
+        nc.vector.tensor_tensor(side_t[0][:], side_t[0][:], wgs_t[0][:], ALU.mult)
         for h in range(HALVES):
             nc.vector.tensor_copy(v_w[last][:, half(h)], tab_w[last][:].bitcast(U32).indirect(idx[:, list_half(h)]))
             product(0, h)
         nc.sync.dma_start(out=slope_t[:], in_=slope.rearrange("(g p t) -> p g t", p=P, t=PACK))
         nc.sync.dma_start(out=swell_t[:], in_=swell.rearrange("(g p t) -> p g t", p=P, t=PACK))
-        load_slice(1)
+        load_side(1)
+        load_page(1)
+        for h in range(HALVES):
+            product(1, h)
+        load_side(2)
         load_w1(1, 0)
-        round_w1(1, 0)
-        load_slice(2)
+        load_page(2)
         for a in range(1, K_PASSES):
             load_w1(1, a)
-            round_w1(1, a)
+        load_side(3)
 
         tiles = [(c, h) for h in range(HALVES) for c in range(N_TILES)]
         sums = {}
+        late_bf = []
         whole, whole_list = slice(0, S), slice(0, S // 16)
         for s in range(SLICES):
             g, t = divmod(s, PACK)
@@ -333,14 +346,15 @@ def tile_list_groove_noise_page_kernel(
             else:
                 scatter(s, whole, whole_list)
             if s + 3 < SLICES:
-                load_slice(s + 3)
-            nc.sync.dma_start(out=out_1_rows[g, t], in_=page_t[s][:])
+                load_page(s + 3)
+            if s + 4 < SLICES:
+                load_side(s + 4)
+            nc.scalar.dma_start(out=out_1_rows[g, t], in_=page_t[s][:])
             if s == 2:
                 prepare_w2_w3()
-                nc.vector.tensor_scalar(out=neg_lift[:], in0=lift_t[:], scalar1=-1.0, scalar2=None, op0=ALU.mult)
-            if s == PACK - 1:
-                for a in range(K_PASSES):
-                    quantize_w1(1, a)
+            if s == 2:
+                quantize_w1(1, 0, late_bf[0][:])
+                quantize_w1(1, 1, late_bf[1][:])
             if s == PACK:
                 for h in range(HALVES):
                     make_x(0, h)
@@ -348,16 +362,26 @@ def tile_list_groove_noise_page_kernel(
                     quantize_x(0, h)
                 for h in range(HALVES):
                     page_planes(0, h)
+                round_w2()
             if s == SLICES - 2:
                 quantize_w2()
-            if s + 1 < SLICES:
+                neg_lift = keep.tile([P, N_TILES], F32, name="neg_lift", tag="v_sc", align_bytes=64)
+                nc.vector.tensor_scalar(out=neg_lift[:], in0=lift_t[:], scalar1=-1.0, scalar2=None, op0=ALU.mult)
+            if s + 2 < SLICES:
                 for h in range(HALVES):
-                    product(s + 1, h)
+                    product(s + 2, h)
             if s == SLICES - 2:
                 for i, (c, h) in enumerate(tiles[:4]):
                     for which in range(2):
                         sums[c, h, which] = new_bank((4 + 2 * i + which) % 8)
                         score_pass(sums[c, h, which], which, c, h, 0)
+            if s == 0:
+                late_bf.append(keep.tile([P, PASS * PACK], BF16, name="late_bf0", tag="h0", align_bytes=64))
+                round_w1(1, 0, late_bf[0][:])
+            if s == 1:
+                late_bf.append(keep.tile([P, 2 * PASS * PACK], BF16, name="late_bf1", tag="h1", align_bytes=64))
+                for a in (1, 2):
+                    round_w1(1, a, late_bf[1][:, (a - 1) * PASS * PACK : a * PASS * PACK])
             if s + 1 < SLICES:
                 fetch(s, whole, whole_list)
                 for h in range(HALVES):

@@ -28,7 +28,7 @@ N_TILES = N // P
 HALVES = 2
 QUADS = 4
 QUAD = 32
-H_TAGS = ("h0", "h1", "h2", "h3", "h0", "h1", "big2", "h3")
+H_TAGS = ("h0", "h1", "h2", "h3", "h0", "h1", "h6", "h3")
 
 
 def tile_list_groove_noise_page_kernel(
@@ -117,10 +117,9 @@ def tile_list_groove_noise_page_kernel(
         load_w1(0, 2)
         tab_w = []
         for a in range(K_PASSES):
-            if a == K_PASSES - 1:
-                load_side(0)
             tab_w.append(keep.tile([P, T], I32, name=f"tab_w{a}", tag=f"big{a}", align_bytes=64))
             nc.sync.dma_start(out=tab_w[a][:], in_=tab_words[a].rearrange("p t i -> p (t i)").bitcast(I32))
+        load_side(0)
         load_page(0)
 
         ident = keep.tile([P, P], F32, name="ident")
@@ -183,16 +182,28 @@ def tile_list_groove_noise_page_kernel(
         def scatter(s, cols, list_cols):
             nc.vector.tensor_copy(page_t[s][:].indirect(idx2[:, list_cols]), h_t[s][:, cols])
 
-        picked, bent, page_bf = {}, {}, {}
+        picked, page_bf = {}, {}
 
         def fetch(s, cols, list_cols):
             g, t = divmod(s, PACK)
             if g not in picked:
-                picked[g] = keep.tile([P, PACK, PICK], F32, name=f"picked{g}", tag="big0", align_bytes=64)
-                bent[g] = keep.tile([P, PACK, PICK], F32, name=f"bent{g}", tag="big1", align_bytes=64)
-            nc.vector.tensor_copy(picked[g][:, t, cols], page_t[s][:].indirect(idx3[:, list_cols]))
-            nc.scalar.activation(bent[g][:, t, cols], picked[g][:, t, cols], ACT.Tanh, scale=slope_t[:, g, t : t + 1])
-            nc.scalar.activation(bent[g][:, t, cols], bent[g][:, t, cols], ACT.Copy, scale=swell_t[:, g, t : t + 1])
+                picked[g] = keep.tile([P, PACK, PICK], F32, name=f"picked{g}", tag=f"big{g}", align_bytes=64)
+            r = picked[g][:, t, cols]
+            bent = ring.tile([P, r.shape[1]], F32, name="bent", tag="bent")
+            nc.vector.tensor_copy(r, page_t[s][:].indirect(idx3[:, list_cols]))
+            nc.scalar.activation(bent[:], r, ACT.Tanh, scale=slope_t[:, g, t : t + 1])
+            return r, bent
+
+        def bend_aside(s, r, bent):
+            g, t = divmod(s, PACK)
+            nc.scalar.activation(bent[:], bent[:], ACT.Copy, scale=swell_t[:, g, t : t + 1])
+            nc.gpsimd.tensor_tensor(r, r, bent[:], ALU.add)
+
+        def bend_on_vector(s, r, bent):
+            g, t = divmod(s, PACK)
+            nc.vector.scalar_tensor_tensor(
+                out=r, in0=bent[:], scalar=swell_t[:, g, t : t + 1], in1=r, op0=ALU.mult, op1=ALU.add
+            )
 
         HALF_T2 = T2 // 2
         pairs = {}
@@ -218,7 +229,7 @@ def tile_list_groove_noise_page_kernel(
         def page_planes(g, h):
             if g not in y_codes:
                 if g == 0:
-                    y_codes[g] = keep.tile([P, T2], I32, name="y_codes0", tag="h0", align_bytes=64)
+                    y_codes[g] = keep.tile([P, T2], I32, name="y_codes0", tag="h6", align_bytes=64)
                 else:
                     y_codes[g] = ring.tile([P, T2], I32, name="y_codes1", tag="page", bufs=4, align_bytes=64)
                 y_sc[g] = keep.tile([P, T2], U8, name=f"y_sc{g}", tag="y_sc", align_bytes=64)
@@ -245,12 +256,10 @@ def tile_list_groove_noise_page_kernel(
 
         def make_x(g, h):
             if g not in x_bf:
-                x_bf[g] = keep.tile([P, PICK * PACK], BF16, name=f"x_bf{g}", tag="h0", align_bytes=64)
-            nc.vector.tensor_tensor(
-                x_bf[g][:, h * BANK * PACK : (h + 1) * BANK * PACK].rearrange("p (c i t) -> p c t i", i=2, t=PACK),
-                picked[g][:, :, half(h)].rearrange("p t (c i) -> p c t i", i=2),
-                bent[g][:, :, half(h)].rearrange("p t (c i) -> p c t i", i=2),
-                ALU.add,
+                x_bf[g] = keep.tile([P, PICK * PACK], BF16, name=f"x_bf{g}", tag="h6", align_bytes=64)
+            nc.vector.tensor_copy(
+                x_bf[g][:, h * BANK * PACK : (h + 1) * BANK * PACK].rearrange("p (c i t) -> p c t i", i=4, t=PACK),
+                picked[g][:, :, half(h)].rearrange("p t (c i) -> p c t i", i=4),
             )
 
         def quantize_x(g, h):
@@ -288,7 +297,7 @@ def tile_list_groove_noise_page_kernel(
                 )
 
         def quantize_w2():
-            w2_codes.append(keep.tile([P, GROUPS * N], U32, name="w2_codes", tag="h6", align_bytes=64))
+            w2_codes.append(keep.tile([P, GROUPS * N], U32, name="w2_codes", tag="big0", align_bytes=64))
             for lo, hi in ((0, 512), (512, 768)):
                 nc.vector.quantize_mx(
                     out=w2_codes[0][:, lo:hi].bitcast(FP8X4), scales=w2_sc[:, lo:hi], in_=w2_bf[0][:, lo * PACK : hi * PACK]
@@ -317,10 +326,12 @@ def tile_list_groove_noise_page_kernel(
             nc.sync.dma_start(out=out_0[c * P : (c + 1) * P, half(h)], in_=y[:])
 
         last = K_PASSES - 1
-        nc.vector.tensor_tensor(side_t[0][:], side_t[0][:], wgs_t[0][:], ALU.mult)
         for h in range(HALVES):
+            nc.gpsimd.tensor_tensor(side_t[0][:, half(h)], side_t[0][:, half(h)], wgs_t[0][:, half(h)], ALU.mult)
             nc.vector.tensor_copy(v_w[last][:, half(h)], tab_w[last][:].bitcast(U32).indirect(idx[:, list_half(h)]))
+        for h in range(HALVES):
             product(0, h)
+            scatter(0, half(h), list_half(h))
         nc.sync.dma_start(out=slope_t[:], in_=slope.rearrange("(g p t) -> p g t", p=P, t=PACK))
         nc.sync.dma_start(out=swell_t[:], in_=swell.rearrange("(g p t) -> p g t", p=P, t=PACK))
         load_side(1)
@@ -329,21 +340,18 @@ def tile_list_groove_noise_page_kernel(
             product(1, h)
         load_side(2)
         load_w1(1, 0)
+        load_w1(1, 1)
         load_page(2)
-        for a in range(1, K_PASSES):
-            load_w1(1, a)
+        load_w1(1, 2)
         load_side(3)
 
         tiles = [(c, h) for h in range(HALVES) for c in range(N_TILES)]
         sums = {}
         late_bf = []
         whole, whole_list = slice(0, S), slice(0, S // 16)
-        for s in range(SLICES):
+        for s in range(SLICES - 1):
             g, t = divmod(s, PACK)
-            if s == 0:
-                for h in range(HALVES):
-                    scatter(s, half(h), list_half(h))
-            else:
+            if s > 0:
                 scatter(s, whole, whole_list)
             if s + 3 < SLICES:
                 load_page(s + 3)
@@ -352,48 +360,48 @@ def tile_list_groove_noise_page_kernel(
             nc.scalar.dma_start(out=out_1_rows[g, t], in_=page_t[s][:])
             if s == 2:
                 prepare_w2_w3()
-            if s == 2:
                 quantize_w1(1, 0, late_bf[0][:])
-                quantize_w1(1, 1, late_bf[1][:])
-            if s == PACK:
+                quantize_w1(1, 2, late_bf[1][:])
+            if s == SLICES - 2:
                 for h in range(HALVES):
                     make_x(0, h)
                 for h in range(HALVES):
                     quantize_x(0, h)
+                quantize_w2()
                 for h in range(HALVES):
                     page_planes(0, h)
-                round_w2()
-            if s == SLICES - 2:
-                quantize_w2()
                 neg_lift = keep.tile([P, N_TILES], F32, name="neg_lift", tag="v_sc", align_bytes=64)
                 nc.vector.tensor_scalar(out=neg_lift[:], in0=lift_t[:], scalar1=-1.0, scalar2=None, op0=ALU.mult)
-            if s + 2 < SLICES:
-                for h in range(HALVES):
-                    product(s + 2, h)
-            if s == SLICES - 2:
                 for i, (c, h) in enumerate(tiles[:4]):
                     for which in range(2):
                         sums[c, h, which] = new_bank((4 + 2 * i + which) % 8)
                         score_pass(sums[c, h, which], which, c, h, 0)
-            if s == 0:
-                late_bf.append(keep.tile([P, PASS * PACK], BF16, name="late_bf0", tag="h0", align_bytes=64))
-                round_w1(1, 0, late_bf[0][:])
-            if s == 1:
-                late_bf.append(keep.tile([P, 2 * PASS * PACK], BF16, name="late_bf1", tag="h1", align_bytes=64))
-                for a in (1, 2):
-                    round_w1(1, a, late_bf[1][:, (a - 1) * PASS * PACK : a * PASS * PACK])
-            if s + 1 < SLICES:
-                fetch(s, whole, whole_list)
+            if s + 2 < SLICES:
                 for h in range(HALVES):
-                    round_page(s, h)
-            if s == PACK - 1:
+                    product(s + 2, h)
+            bend_aside(s, *fetch(s, whole, whole_list))
+            if s == 0:
+                late_bf.append(keep.tile([P, 2 * PASS * PACK], BF16, name="late_bf0", tag="h0", align_bytes=64))
+                for a in range(2):
+                    round_w1(1, a, late_bf[0][:, a * PASS * PACK : (a + 1) * PASS * PACK])
+            if s == 1:
+                late_bf.append(keep.tile([P, PASS * PACK], BF16, name="late_bf1", tag="h1", align_bytes=64))
+                round_w1(1, 2, late_bf[1][:])
+            if s == PACK:
                 for h in range(HALVES):
                     weave_page(0, h)
+            if s == PACK + 1:
+                round_w2()
+            for done in {0: (), 1: (0,), 2: (1, 2), 3: (3,), 4: (), 5: (4,), 6: (5, 6)}[s]:
+                for h in range(HALVES):
+                    round_page(done, h)
 
         s, g = SLICES - 1, GROUPS - 1
+        scatter(s, whole, whole_list)
+        nc.scalar.dma_start(out=out_1_rows[g, PACK - 1], in_=page_t[s][:])
+        fetched = [fetch(s, half(h), list_half(h)) for h in range(HALVES)]
         for h in range(HALVES):
-            fetch(s, half(h), list_half(h))
-        for h in range(HALVES):
+            bend_on_vector(s, *fetched[h])
             make_x(g, h)
             quantize_x(g, h)
         for i, (c, h) in enumerate(tiles):

@@ -105,22 +105,22 @@ def tile_list_groove_noise_page_kernel(
         wgs_raw = keep.tile([P, S], F32, name="wgs_raw", tag="h6", align_bytes=64)
         nc.sync.dma_start(out=wgs_raw[:], in_=wgs)
         load_w1(0, 0)
+        load_w1(0, 1)
         for q in range(QUADS):
-            nc.sync.dma_start(
+            nc.gpsimd.dma_start(
                 out=tab_sc[QUAD * q : QUAD * q + 4 * K_PASSES, :].bitcast(I32),
                 in_=tab_scales[:, 4 * q : 4 * q + 4, :].bitcast(I32),
             )
         nc.sync.dma_start(idx[:], offs)
-        nc.sync.dma_start(idx2[:], offs2)
-        nc.sync.dma_start(idx3[:], offs3)
-        load_w1(0, 1)
         load_w1(0, 2)
         tab_w = []
         for a in range(K_PASSES):
             tab_w.append(keep.tile([P, T], I32, name=f"tab_w{a}", tag=f"big{a}", align_bytes=64))
             nc.sync.dma_start(out=tab_w[a][:], in_=tab_words[a].rearrange("p t i -> p (t i)").bitcast(I32))
+        nc.sync.dma_start(idx2[:], offs2)
         load_side(0)
         load_page(0)
+        nc.sync.dma_start(idx3[:], offs3)
 
         ident = keep.tile([P, P], F32, name="ident")
         make_identity(nc, ident[:])

from contextlib import ExitStack

import concourse.mybir as mybir
from concourse.masks import make_identity

T, S, T2, PICK, K, H, N = 4096, 1024, 2048, 1024, 1536, 1024, 384
FLOPS = 2 * K * H * S + 2 * 2 * H * N * PICK

F32 = mybir.dt.float32
BF16 = mybir.dt.bfloat16
I32 = mybir.dt.int32
U32 = mybir.dt.uint32
U16 = mybir.dt.uint16
U8 = mybir.dt.uint8
FP8X4 = mybir.dt.float8_e4m3fn_x4
FP4X4 = mybir.dt.float4_e2m1fn_x4
ALU = mybir.AluOpType
ACT = mybir.ActivationFunctionType

P = 128
PACK = 4
PASS = P * PACK
BANK = 512
K_PASSES = K // PASS
GROUPS = H // PASS
SLICES = GROUPS * PACK
N_TILES = N // P
HALVES = 2
QUADS = 4
QUAD = 32
H_TAGS = ("h0", "h1", "h2", "h3", "h0", "h1", "h6", "h3")


def tile_list_groove_noise_page_kernel(
    tc, tab_words, tab_scales, offs, offs2, offs3, w1, side, wgs, page0, slope, swell, w2, w3_words, w3_scales, lift,
    out_0, out_1, out_2, out_3,
):
    nc = tc.nc
    side_rows = side.rearrange("(g p t) j -> g t p j", p=P, t=PACK)
    page0_rows = page0.rearrange("(g p t) m -> g t p m", p=P, t=PACK)
    out_1_rows = out_1.rearrange("(g p t) m -> g t p m", p=P, t=PACK)

    with ExitStack() as ctx:
        lists = ctx.enter_context(tc.tile_pool(name="lists", bufs=1))
        keep = ctx.enter_context(tc.tile_pool(name="keep", bufs=1))
        ring = ctx.enter_context(tc.tile_pool(name="ring", bufs=2))
        psum = ctx.enter_context(tc.psum_pool(name="psum", bufs=1))

        idx = lists.tile([P, S // 16], U16, name="idx")
        idx2 = lists.tile([P, S // 16], U16, name="idx2")
        idx3 = lists.tile([P, PICK // 16], U16, name="idx3")

        def half(h):
            return slice(h * BANK, (h + 1) * BANK)

        def list_half(h):
            return slice(h * BANK // 16, (h + 1) * BANK // 16)

        tab_sc = keep.tile([P, T], U8, name="tab_sc", tag="h3", align_bytes=64)
        w3_sc = keep.tile([P, GROUPS, N], U8, name="w3_sc", align_bytes=64)
        nc.vector.memset(tab_sc[:].bitcast(I32), 0)
        nc.vector.memset(w3_sc[:].bitcast(I32), 0)
        slope_t = keep.tile([P, GROUPS, PACK], F32, name="slope_t")
        swell_t = keep.tile([P, GROUPS, PACK], F32, name="swell_t")
        lift_t = keep.tile([P, N_TILES], F32, name="lift_t")

        w1_raw, w1_codes, w1_sc = {}, {}, {}

        def load_w1(g, a):
            w1_raw[g, a] = ring.tile([P, PACK, PASS], F32, name="w_raw", tag="w_raw", bufs=3)
            rows = w1[a * PASS : (a + 1) * PASS, g * PASS : (g + 1) * PASS]
            nc.sync.dma_start(out=w1_raw[g, a][:], in_=rows.rearrange("(p i) r -> p i r", i=PACK))

        def round_w1(g, a, grouped):
            nc.scalar.copy(
                out=grouped.rearrange("p (t q i) -> p q i t", t=PACK, i=PACK),
                in_=w1_raw[g, a][:].rearrange("p i (q t) -> p q i t", t=PACK),
            )

        def quantize_w1(g, a, grouped):
            if a == 0:
                tag = "w1_codes0" if g == 0 else "h2"
                w1_codes[g] = keep.tile([P, K_PASSES * PASS], U32, name=f"w1_codes{g}", tag=tag, align_bytes=64)
                w1_sc[g] = keep.tile([P, K_PASSES * PASS], U8, name=f"w1_sc{g}", align_bytes=64)
            cols = slice(a * PASS, a * PASS + grouped.shape[1] // PACK)
            nc.vector.quantize_mx(out=w1_codes[g][:, cols].bitcast(FP8X4), scales=w1_sc[g][:, cols], in_=grouped)

        side_t, page_t = {}, {}
        wgs_t = [keep.tile([P, S], F32, name=f"wgs{t}") for t in range(PACK)]

        def load_side(s):
            side_t[s] = ring.tile([P, S], F32, name="side_t", tag="side_t", bufs=4)
            nc.sync.dma_start(out=side_t[s][:], in_=side_rows[s // PACK, s % PACK])

        def load_page(s):
            page_t[s] = ring.tile([P, T2], F32, name="page", tag="page", bufs=4, align_bytes=64)
            nc.sync.dma_start(out=page_t[s][:], in_=page0_rows[s // PACK, s % PACK])

        banks = [None] * 8

        def new_bank(b):
            banks[b] = psum.tile([P, BANK], F32, name=f"bank{b}", tag=f"bank{b}")
            return banks[b]

        wgs_raw = keep.tile([P, S], F32, name="wgs_raw", tag="h6", align_bytes=64)
        nc.sync.dma_start(out=wgs_raw[:], in_=wgs)
        load_w1(0, 0)
        load_w1(0, 1)
        for q in range(QUADS):
            nc.gpsimd.dma_start(
                out=tab_sc[QUAD * q : QUAD * q + 4 * K_PASSES, :].bitcast(I32),
                in_=tab_scales[:, 4 * q : 4 * q + 4, :].bitcast(I32),
            )
        nc.sync.dma_start(idx[:], offs)
        load_w1(0, 2)
        tab_w = []
        for a in range(K_PASSES):
            tab_w.append(keep.tile([P, T], I32, name=f"tab_w{a}", tag=f"big{a}", align_bytes=64))
            nc.sync.dma_start(out=tab_w[a][:], in_=tab_words[a].rearrange("p t i -> p (t i)").bitcast(I32))
        nc.sync.dma_start(idx2[:], offs2)
        load_side(0)
        load_page(0)
        nc.sync.dma_start(idx3[:], offs3)

        ident = keep.tile([P, P], F32, name="ident")
        make_identity(nc, ident[:])
        turned = []
        for h in range(HALVES):
            acc = new_bank(4 + h)
            for b in range(4):
                nc.tensor.transpose(acc[:, b * P : (b + 1) * P], wgs_raw[:, h * BANK + b * P : h * BANK + (b + 1) * P], ident[:])
            turned.append(keep.tile([P, 4 * PACK * P], F32, name=f"turned{h}", tag=f"pairs{h}", align_bytes=64))
            for b in range(4):
                rows = acc[:, b * P : (b + 1) * P].rearrange("p (q t) -> p t q", t=PACK)
                nc.vector.tensor_copy(
                    turned[h][:, b * PASS : (b + 1) * PASS].rearrange("p (t r q) -> p t r q", t=PACK, r=QUADS),
                    rows.unsqueeze(2).broadcast_to([P, PACK, QUADS, QUAD]),
                )

        v_sc = keep.tile([P, S], U8, name="v_sc", tag="v_sc", align_bytes=64)
        nc.vector.tensor_copy(v_sc[:], tab_sc[:].indirect(idx[:]))
        for a in range(K_PASSES):
            grouped = ring.tile([P, PASS * PACK], BF16, name="w_bf", tag="w_bf", align_bytes=64)
            round_w1(0, a, grouped[:])
            quantize_w1(0, a, grouped[:])
        for t in range(PACK):
            for h in range(HALVES):
                acc = new_bank(4 + (2 + HALVES * t + h) % 4)
                for b in range(4):
                    cols = slice(b * PASS + t * P, b * PASS + (t + 1) * P)
                    nc.tensor.transpose(acc[:, b * P : (b + 1) * P], turned[h][:, cols], ident[:])
                nc.scalar.copy(out=wgs_t[t][:, half(h)], in_=acc[:])
        v_w = [keep.tile([P, S], U32, name=f"v_w{a}", align_bytes=64) for a in range(K_PASSES)]
        for a in range(K_PASSES - 1):
            nc.vector.tensor_copy(v_w[a][:], tab_w[a][:].bitcast(U32).indirect(idx[:]))

        h_t = {}

        def product(s, h):
            g, t = divmod(s, PACK)
            if s not in h_t:
                h_t[s] = keep.tile([P, S], F32, name=f"h{s}", tag=H_TAGS[s], align_bytes=64)
            acc = new_bank(2 * (s % 2) + h)
            for a in range(K_PASSES):
                nc.tensor.matmul_mx(
                    out=acc[:],
                    lhsT=w1_codes[g][:, a * PASS + t * P : a * PASS + (t + 1) * P].bitcast(FP8X4),
                    lhsT_scale=w1_sc[g][:, a * PASS + t * P : a * PASS + (t + 1) * P],
                    rhs=v_w[a][:, half(h)].bitcast(FP8X4),
                    rhs_scale=v_sc[4 * a : P, half(h)],
                    start=(a == 0),
                    stop=(a == K_PASSES - 1),
                )
            if s == 0:
                nc.vector.tensor_tensor(h_t[s][:, half(h)], acc[:], side_t[s][:, half(h)], ALU.mult)
                return
            nc.scalar.copy(out=h_t[s][:, half(h)], in_=acc[:])
            if h == 1:
                nc.gpsimd.tensor_tensor(h_t[s][:], h_t[s][:], wgs_t[t][:], ALU.mult)
                nc.gpsimd.tensor_tensor(h_t[s][:], h_t[s][:], side_t[s][:], ALU.mult)

        def scatter(s, cols, list_cols):
            nc.vector.tensor_copy(page_t[s][:].indirect(idx2[:, list_cols]), h_t[s][:, cols])

        picked, page_bf = {}, {}

        def fetch(s, cols, list_cols):
            g, t = divmod(s, PACK)
            if g not in picked:
                picked[g] = keep.tile([P, PACK, PICK], F32, name=f"picked{g}", tag=f"big{g}", align_bytes=64)
            r = picked[g][:, t, cols]
            bent = ring.tile([P, r.shape[1]], F32, name="bent", tag="bent")
            nc.vector.tensor_copy(r, page_t[s][:].indirect(idx3[:, list_cols]))
            nc.scalar.activation(bent[:], r, ACT.Tanh, scale=slope_t[:, g, t : t + 1])
            return r, bent

        def bend_aside(s, r, bent):
            g, t = divmod(s, PACK)
            nc.scalar.activation(bent[:], bent[:], ACT.Copy, scale=swell_t[:, g, t : t + 1])
            nc.gpsimd.tensor_tensor(r, r, bent[:], ALU.add)

        def bend_on_vector(s, r, bent):
            g, t = divmod(s, PACK)
            nc.vector.scalar_tensor_tensor(
                out=r, in0=bent[:], scalar=swell_t[:, g, t : t + 1], in1=r, op0=ALU.mult, op1=ALU.add
            )

        HALF_T2 = T2 // 2
        pairs = {}

        def round_page(s, h):
            g, t = divmod(s, PACK)
            if (g, h) not in pairs:
                pairs[g, h] = keep.tile([P, HALF_T2 * PACK], BF16, name=f"pairs{g}{h}", tag=f"pairs{h}", align_bytes=64)
            by_pair = pairs[g, h][:].rearrange("p (u m e) -> p u m e", u=2, e=2)
            nc.scalar.copy(out=by_pair[:, t // 2, :, t % 2], in_=page_t[s][:, h * HALF_T2 : (h + 1) * HALF_T2])

        def weave_page(g, h):
            if g not in page_bf:
                page_bf[g] = keep.tile([P, T2 * PACK], BF16, name=f"page_bf{g}", tag="big2", align_bytes=64)
            woven = page_bf[g][:, h * HALF_T2 * PACK : (h + 1) * HALF_T2 * PACK]
            nc.scalar.copy(
                out=woven.bitcast(F32).rearrange("p (c i u) -> p c u i", i=2, u=2),
                in_=pairs[g, h][:].bitcast(F32).rearrange("p (u c i) -> p c u i", u=2, i=2),
            )

        y_codes, y_sc = {}, {}

        def page_planes(g, h):
            if g not in y_codes:
                if g == 0:
                    y_codes[g] = keep.tile([P, T2], I32, name="y_codes0", tag="h6", align_bytes=64)
                else:
                    y_codes[g] = ring.tile([P, T2], I32, name="y_codes1", tag="page", bufs=4, align_bytes=64)
                y_sc[g] = keep.tile([P, T2], U8, name=f"y_sc{g}", tag="y_sc", align_bytes=64)
            cols = slice(h * HALF_T2, (h + 1) * HALF_T2)
            nc.vector.quantize_mx(
                out=y_codes[g][:, cols].bitcast(FP8X4),
                scales=y_sc[g][:, cols],
                in_=page_bf[g][:, h * HALF_T2 * PACK : (h + 1) * HALF_T2 * PACK],
            )
            nc.sync.dma_start(
                out=out_2[g].rearrange("p m t -> p (m t)").bitcast(I32)[:, cols], in_=y_codes[g][:, cols]
            )
            if h == 1:
                for q in range(QUADS):
                    nc.sync.dma_start(
                        out=out_3[g, 4 * q : 4 * q + 4, :].bitcast(I32),
                        in_=y_sc[g][QUAD * q : QUAD * q + 4, :].bitcast(I32),
                    )

        x_codes = [keep.tile([P, PICK], U32, name=f"x_codes{g}", align_bytes=64) for g in range(GROUPS)]
        x_sc = [keep.tile([P, PICK], U8, name=f"x_sc{g}", align_bytes=64) for g in range(GROUPS)]

        x_bf = {}

        def make_x(g, h):
            if g not in x_bf:
                x_bf[g] = keep.tile([P, PICK * PACK], BF16, name=f"x_bf{g}", tag="h6", align_bytes=64)
            nc.vector.tensor_copy(
                x_bf[g][:, h * BANK * PACK : (h + 1) * BANK * PACK].rearrange("p (c i t) -> p c t i", i=4, t=PACK),
                picked[g][:, :, half(h)].rearrange("p t (c i) -> p c t i", i=4),
            )

        def quantize_x(g, h):
            nc.vector.quantize_mx(
                out=x_codes[g][:, half(h)].bitcast(FP8X4),
                scales=x_sc[g][:, half(h)],
                in_=x_bf[g][:, h * BANK * PACK : (h + 1) * BANK * PACK],
            )

        w2_codes = []
        w2_sc = keep.tile([P, GROUPS * N], U8, name="w2_sc", align_bytes=64)
        w3_w = keep.tile([P, GROUPS, 2 * N], U8, name="w3_w", align_bytes=64)
        w2_raw, w2_bf = [], []

        def round_w2():
            w2_bf.append(keep.tile([P, GROUPS * N * PACK], BF16, name="w2_bf", tag="h0", align_bytes=64))
            for g in range(GROUPS):
                nc.scalar.copy(
                    out=w2_bf[0][:, g * N * PACK : (g + 1) * N * PACK].rearrange("p (c n i) -> p c i n", n=4, i=PACK),
                    in_=w2_raw[g][:].rearrange("p i (c n) -> p c i n", n=4),
                )

        def prepare_w2_w3():
            for g in range(GROUPS):
                w2_raw.append(ring.tile([P, PACK, N], F32, name="w_raw", tag="w_raw", bufs=3))
                rows = w2[g * PASS : (g + 1) * PASS, :]
                nc.sync.dma_start(out=w2_raw[g][:], in_=rows.rearrange("(p i) n -> p i n", i=PACK))
            nc.sync.dma_start(out=w3_w[:].bitcast(I32), in_=w3_words.bitcast(I32).rearrange("g p w -> p g w"))
            with nc.allow_non_contiguous_dma(reason="one value of lift a partition"):
                nc.sync.dma_start(out=lift_t[:], in_=lift.rearrange("(c p) -> p c", p=P))
            for q in range(QUADS):
                nc.sync.dma_start(
                    out=w3_sc[QUAD * q : QUAD * q + 4, :, :].bitcast(I32),
                    in_=w3_scales[:, 4 * q : 4 * q + 4, :].bitcast(I32).rearrange("g r n -> r g n"),
                )

        def quantize_w2():
            w2_codes.append(keep.tile([P, GROUPS * N], U32, name="w2_codes", tag="big0", align_bytes=64))
            for lo, hi in ((0, 512), (512, 768)):
                nc.vector.quantize_mx(
                    out=w2_codes[0][:, lo:hi].bitcast(FP8X4), scales=w2_sc[:, lo:hi], in_=w2_bf[0][:, lo * PACK : hi * PACK]
                )

        def score_pass(acc, which, c, h, g):
            if which == 0:
                cols = slice(g * N + c * P, g * N + (c + 1) * P)
                lhsT, lhsT_scale = w2_codes[0][:, cols].bitcast(FP8X4), w2_sc[:, cols]
            else:
                lhsT = w3_w[:, g, 2 * c * P : 2 * (c + 1) * P].bitcast(FP4X4)
                lhsT_scale = w3_sc[:, g, c * P : (c + 1) * P]
            nc.tensor.matmul_mx(
                out=acc[:], lhsT=lhsT, lhsT_scale=lhsT_scale,
                rhs=x_codes[g][:, half(h)].bitcast(FP8X4), rhs_scale=x_sc[g][:, half(h)],
                start=(g == 0), stop=(g == GROUPS - 1),
            )

        def score_out(c, h, first, second):
            neg_second = ring.tile([P, BANK], F32, name="neg_second", tag="w_raw", bufs=3)
            nc.scalar.activation(neg_second[:], second[:], ACT.Copy, scale=-1.0)
            y = ring.tile([P, BANK], F32, name="y", tag="side_t", bufs=4)
            nc.vector.scalar_tensor_tensor(
                out=y[:], in0=neg_second[:], scalar=neg_lift[:, c : c + 1], in1=first[:], op0=ALU.min, op1=ALU.add
            )
            nc.sync.dma_start(out=out_0[c * P : (c + 1) * P, half(h)], in_=y[:])

        last = K_PASSES - 1
        for h in range(HALVES):
            nc.gpsimd.tensor_tensor(side_t[0][:, half(h)], side_t[0][:, half(h)], wgs_t[0][:, half(h)], ALU.mult)
            nc.vector.tensor_copy(v_w[last][:, half(h)], tab_w[last][:].bitcast(U32).indirect(idx[:, list_half(h)]))
        for h in range(HALVES):
            product(0, h)
            scatter(0, half(h), list_half(h))
        nc.sync.dma_start(out=slope_t[:], in_=slope.rearrange("(g p t) -> p g t", p=P, t=PACK))
        nc.sync.dma_start(out=swell_t[:], in_=swell.rearrange("(g p t) -> p g t", p=P, t=PACK))
        load_side(1)
        load_page(1)
        for h in range(HALVES):
            product(1, h)
        load_side(2)
        load_w1(1, 0)
        load_w1(1, 1)
        load_page(2)
        load_w1(1, 2)
        load_side(3)

        tiles = [(c, h) for h in range(HALVES) for c in range(N_TILES)]
        sums = {}
        late_bf = []
        whole, whole_list = slice(0, S), slice(0, S // 16)
        for s in range(SLICES - 1):
            g, t = divmod(s, PACK)
            if s > 0:
                scatter(s, whole, whole_list)
            if s + 3 < SLICES:
                load_page(s + 3)
            if s + 4 < SLICES:
                load_side(s + 4)
            nc.scalar.dma_start(out=out_1_rows[g, t], in_=page_t[s][:])
            if s == 2:
                prepare_w2_w3()
                quantize_w1(1, 0, late_bf[0][:])
                quantize_w1(1, 2, late_bf[1][:])
            if s == SLICES - 2:
                for h in range(HALVES):
                    make_x(0, h)
                for h in range(HALVES):
                    quantize_x(0, h)
                quantize_w2()
                for h in range(HALVES):
                    page_planes(0, h)
                neg_lift = keep.tile([P, N_TILES], F32, name="neg_lift", tag="v_sc", align_bytes=64)
                nc.vector.tensor_scalar(out=neg_lift[:], in0=lift_t[:], scalar1=-1.0, scalar2=None, op0=ALU.mult)
                for i, (c, h) in enumerate(tiles[:4]):
                    for which in range(2):
                        sums[c, h, which] = new_bank((4 + 2 * i + which) % 8)
                        score_pass(sums[c, h, which], which, c, h, 0)
            if s + 2 < SLICES:
                for h in range(HALVES):
                    product(s + 2, h)
            bend_aside(s, *fetch(s, whole, whole_list))
            if s == 0:
                late_bf.append(keep.tile([P, 2 * PASS * PACK], BF16, name="late_bf0", tag="h0", align_bytes=64))
                for a in range(2):
                    round_w1(1, a, late_bf[0][:, a * PASS * PACK : (a + 1) * PASS * PACK])
            if s == 1:
                late_bf.append(keep.tile([P, PASS * PACK], BF16, name="late_bf1", tag="h1", align_bytes=64))
                round_w1(1, 2, late_bf[1][:])
            if s == PACK:
                for h in range(HALVES):
                    weave_page(0, h)
            if s == PACK + 1:
                round_w2()
            for done in {0: (), 1: (0,), 2: (1, 2), 3: (3,), 4: (), 5: (4,), 6: (5, 6)}[s]:
                for h in range(HALVES):
                    round_page(done, h)

        s, g = SLICES - 1, GROUPS - 1
        scatter(s, whole, whole_list)
        nc.scalar.dma_start(out=out_1_rows[g, PACK - 1], in_=page_t[s][:])
        fetched = [fetch(s, half(h), list_half(h)) for h in range(HALVES)]
        for h in range(HALVES):
            bend_on_vector(s, *fetched[h])
            make_x(g, h)
            quantize_x(g, h)
        for i, (c, h) in enumerate(tiles):
            for which in range(2):
                if i >= 4:
                    sums[c, h, which] = new_bank((4 + 2 * i + which) % 8)
                    score_pass(sums[c, h, which], which, c, h, 0)
                score_pass(sums[c, h, which], which, c, h, 1)
            score_out(c, h, sums[c, h, 0], sums[c, h, 1])
            if i in (0, 2):
                round_page(s, i // 2)
                weave_page(g, i // 2)
                page_planes(g, i // 2)
